import numpy as np
import ml_dtypes


def mxq(x, axis, fmt="e4m3"):
    dtype, down = {"e4m3": (ml_dtypes.float8_e4m3fn, 7), "e5m2": (ml_dtypes.float8_e5m2, 14)}[fmt]
    v = np.moveaxis(np.asarray(x, np.float32).astype(ml_dtypes.bfloat16).astype(np.float64), axis, -1)
    blocks = v.reshape(v.shape[:-1] + (-1, 32))
    amax = np.abs(blocks).max(-1, keepdims=True)
    byte = np.maximum(np.where(amax > 0, np.frexp(amax)[1] - 1 + 127, 0) - down, 1)
    scale = np.exp2(byte - 127.0)
    codes = (blocks / scale).astype(np.float32).astype(dtype).astype(np.float64)
    return np.moveaxis((codes * scale).reshape(v.shape), -1, axis)


WIDE = False


def mx_kscale(k):
    if not WIDE:
        return np.ones(k)
    levels = np.array([10, -10, 5, -5, 0])
    if k % 512:
        return np.exp2(np.random.permutation(np.resize(levels, k // 32))).repeat(32)
    a = np.empty((k // 512, 16))
    for p in range(k // 512):
        a[p, :8] = np.random.permutation(np.resize(levels, 8))
        for g in range(8):
            far = levels[np.abs(levels - a[p, g]) >= 10]
            a[p, g + 8] = far[np.random.randint(len(far))]
    return np.exp2(a.ravel()).repeat(32)


def f64(x):
    return np.asarray(x).astype(np.float64)


def striped(idx):
    return np.tile(idx.reshape(-1, 16).T, (8, 1)).astype(np.uint16)


def unstriped(offs):
    return offs[:16].T.reshape(-1).astype(np.int64)


E2M1 = np.array([0.0, 0.5, 1.0, 1.5, 2.0, 3.0, 4.0, 6.0, -0.0, -0.5, -1.0, -1.5, -2.0, -3.0, -4.0, -6.0])


def pack_weight(w, fmt):
    k, n = w.shape
    w = f64(np.asarray(w, np.float32).astype(ml_dtypes.bfloat16)).reshape(k // 32, 32, n)
    amax = np.abs(w).max(1)
    if fmt == "e4m3":
        byte = np.frexp(amax)[1] - 1 + 127 - 7
    else:
        mant, ex = np.frexp(amax / 6.0)
        byte = np.where(mant > 0.5, ex, ex - 1) + 127
    byte = np.clip(np.where(amax > 0, byte, 1), 1, 254)
    scaled = (w * np.exp2(127.0 - byte)[:, None, :]).reshape(k, n).astype(np.float32)
    by_word = np.ascontiguousarray(scaled.reshape(k // 512, 128, 4, n).transpose(0, 1, 3, 2))
    if fmt == "e4m3":
        words = by_word.astype(ml_dtypes.float8_e4m3fn).view(np.uint8)
    else:
        c = by_word.astype(ml_dtypes.float4_e2m1fn).view(np.uint8) & 0xF
        words = (c[..., 0::2] | (c[..., 1::2] << 4)).reshape(k // 512, 128, 2 * n)
    return np.ascontiguousarray(words), np.ascontiguousarray(byte.astype(np.uint8).reshape(k // 512, 16, n))


def unpack_weight(words, scales, fmt):
    g, _, n = scales.shape
    words = np.ascontiguousarray(words).reshape(g, 128, n, -1)
    if fmt == "e4m3":
        vals = words.view(ml_dtypes.float8_e4m3fn).astype(np.float64)
    else:
        nib = np.empty((g, 128, n, 4), np.uint8)
        nib[..., 0::2] = words & 0xF
        nib[..., 1::2] = words >> 4
        vals = E2M1[nib]
    vals = vals * np.repeat(np.exp2(scales.astype(np.float64) - 127.0), 8, axis=1)[..., None]
    return vals.transpose(0, 1, 3, 2).reshape(g * 512, n)


def gelu(v):
    return 0.5 * v * (1.0 + np.tanh(np.sqrt(2.0 / np.pi) * (v + 0.044715 * v**3)))


K, KC, T, S, S2 = 1024, 512, 2048, 1024, 512

def setup_inputs():
    n = np.random.standard_normal
    s = mx_kscale(K)[:, None]
    d = {}
    d["tab_words"], d["tab_scales"] = pack_weight(n((K, T)) * s, "e4m3")
    d["offs"] = striped(np.random.permutation(T)[:S])
    d["offs2"] = striped(np.random.permutation(T)[:S2])
    d["w1"] = (2.0 * n((KC, K)) / K / s[:KC] / s.T).astype(np.float32)
    d["w4_words"], d["w4_scales"] = pack_weight(2.0 * n((K - KC, K)) / K / s[KC:] / s.T, "e2m1")
    d["gain"] = np.exp(0.4 * n(S2)).astype(np.float32)
    d["trials"] = n((S2, S)).astype(np.float32)
    return d

def reference(tab_words, tab_scales, offs, offs2, w1, w4_words, w4_scales, gain, trials):
    TW = unpack_weight(tab_words, tab_scales, "e4m3")
    v = TW[:, unstriped(offs)]
    v2 = TW[:, unstriped(offs2)]
    w4 = unpack_weight(w4_words, w4_scales, "e2m1")
    w1q = mxq(f64(w1), 0, "e4m3")
    h = w1q.T @ v[:KC] + w4.T @ v[KC:]
    up = np.maximum(h, 0.0)
    down = np.maximum(-h, 0.0)
    e_up = v2.T @ mxq(up, 0, "e4m3")
    e_down = v2.T @ mxq(down, 0, "e4m3")
    return f64(gain)[:, None] * np.maximum(e_up, e_down) + f64(trials)

@@ -1,0 +1,218 @@
+from contextlib import ExitStack
+
+import concourse.mybir as mybir
+
+K, KC, T, S, S2 = 1024, 512, 2048, 1024, 512
+FLOPS = 2 * K * K * S + 2 * 2 * K * S2 * S
+
+F32 = mybir.dt.float32
+BF16 = mybir.dt.bfloat16
+I32 = mybir.dt.int32
+U32 = mybir.dt.uint32
+U16 = mybir.dt.uint16
+U8 = mybir.dt.uint8
+FP8X4 = mybir.dt.float8_e4m3fn_x4
+FP4X4 = mybir.dt.float4_e2m1fn_x4
+ACT = mybir.ActivationFunctionType
+ALU = mybir.AluOpType
+
+P = 128
+PACK = 4
+CHUNK = 256
+N1 = 128
+PASS0_ROW = 4
+DIRECT = ((0, 0), (1, 0), (2, 0), (3, 0))
+
+
+def tile_list_reed_mouthpiece_fit_kernel(tc, tab_words, tab_scales, offs, offs2, w1, w4_words, w4_scales, gain, trials, out):
+    nc = tc.nc
+    n_chunks = S // CHUNK
+    with ExitStack() as ctx:
+        keep = ctx.enter_context(tc.tile_pool(name="keep", bufs=1))
+        ring = ctx.enter_context(tc.tile_pool(name="ring", bufs=4))
+        ps1 = ctx.enter_context(tc.psum_pool(name="ps1", bufs=4))
+        ps2 = ctx.enter_context(tc.psum_pool(name="ps2", bufs=2))
+
+        reeds = keep.tile([P, S // 16], U16, name="reeds")
+        mouths = keep.tile([P, S2 // 16], U16, name="mouths")
+        tab = [keep.tile([P, T], I32, name="tab%d" % a, align_bytes=64) for a in range(2)]
+        tab_sc = keep.tile([P, T], U8, name="tab_sc", align_bytes=64)
+        w4_raw = keep.tile([P, 2 * K], U8, name="w4_raw", align_bytes=64)
+        w4_sc_raw = keep.tile([P, K], U8, name="w4_sc_raw", align_bytes=64)
+        w4_codes = keep.tile([P, 2 * K], U8, name="w4_codes", align_bytes=64)
+        w4_sc = keep.tile([P, K], U8, name="w4_sc", align_bytes=64)
+        w1_raw = [keep.tile([P, PACK, 256], F32, name="w1_raw%d" % i) for i in range(4)]
+        w1_bf = [keep.tile([P, PACK, P, PACK], BF16, name="w1_bf%d" % b, align_bytes=64) for b in range(2)]
+        w1_codes = [keep.tile([P, 512], U32, name="w1_codes%d" % b, align_bytes=64) for b in range(2)]
+        w1_sc = [keep.tile([P, 512], U8, name="w1_sc%d" % b, align_bytes=64) for b in range(2)]
+        v0 = keep.tile([P, S], U32, name="v0", align_bytes=64)
+        v1 = [keep.tile([P, CHUNK], U32, name="v1_%d" % c, align_bytes=64) for c in range(n_chunks)]
+        v_sc = keep.tile([P, S], U8, name="v_sc", align_bytes=64)
+        u = [keep.tile([P, S2], U32, name="u%d" % a, align_bytes=64) for a in range(2)]
+        u_sc = keep.tile([P, S2], U8, name="u_sc", align_bytes=64)
+        gains = keep.tile([P, 4], F32, name="gains")
+        tri = [keep.tile([P, 4, CHUNK], F32, name="tri%d" % c) for c in range(n_chunks)]
+        warm = keep.tile([P, 2], F32, name="warm")
+
+        nc.vector.memset(tab_sc[:].bitcast(I32), 0)
+        nc.vector.memset(w4_sc_raw[:].bitcast(I32), 0)
+        nc.vector.memset(warm[:, 0:1], 0.0)
+        nc.scalar.activation(out=warm[:, 1:2], in_=warm[:, 0:1], func=ACT.Relu)
+
+        def load_table(a):
+            nc.sync.dma_start(out=tab[a][:], in_=tab_words[a].rearrange("p n t -> p (n t)").bitcast(I32))
+
+        def load_scale_rows(queue, tile, first_row, rows):
+            for r in range(4):
+                queue.dma_start(out=tile[first_row + r : P : 32, :].bitcast(I32), in_=rows[r:16:4, :].bitcast(I32))
+
+        def load_w1(i):
+            nc.sync.dma_start(out=w1_raw[i][:], in_=w1[:, 256 * i : 256 * (i + 1)].rearrange("(p j) c -> p j c", j=PACK))
+
+        def load_trials(c):
+            nc.sync.dma_start(out=tri[c][:], in_=trials[:, CHUNK * c : CHUNK * (c + 1)].rearrange("(g p) j -> p g j", p=P))
+
+        nc.sync.dma_start(reeds[:], offs)
+        nc.sync.dma_start(out=w4_raw[:].bitcast(I32), in_=w4_words[0].bitcast(I32))
+        load_table(0)
+        load_scale_rows(nc.sync, tab_sc, PASS0_ROW, tab_scales[0])
+        load_w1(0)
+        nc.sync.dma_start(mouths[:], offs2)
+        load_w1(1)
+        load_scale_rows(nc.sync, tab_sc, 0, tab_scales[1])
+        load_w1(2)
+        load_w1(3)
+        load_scale_rows(nc.sync, w4_sc_raw, 0, w4_scales[0])
+        load_table(1)
+        with nc.allow_non_contiguous_dma(reason="one gain for each partition"):
+            nc.sync.dma_start(out=gains[:], in_=gain.rearrange("(g p) -> p g", p=P))
+        for c in range(n_chunks):
+            load_trials(c)
+
+
+        def cast_w1(i):
+            b, half = divmod(i, 2)
+            nc.scalar.copy(
+                out=w1_bf[b][:, :, 64 * half : 64 * (half + 1), :].rearrange("p t m j -> p m j t"),
+                in_=w1_raw[i][:].rearrange("p j (m t) -> p m j t", t=PACK),
+            )
+
+        def quant_w1(b):
+            nc.vector.quantize_mx(out=w1_codes[b][:].bitcast(FP8X4), scales=w1_sc[b][:], in_=w1_bf[b][:].rearrange("p t m j -> p (t m j)"))
+
+        def gather(dst, window, offsets):
+            nc.vector.tensor_copy(out=dst, in_=window.indirect(offsets))
+
+        act_codes = {}
+        act_sc = {}
+
+        def stage1(c, b):
+            act = ring.tile([P, 2, CHUNK, PACK], BF16, name="act", align_bytes=64)
+            direct = (c, b) in DIRECT
+            if not direct:
+                hb = ring.tile([P, CHUNK, PACK], BF16, name="hb", align_bytes=64)
+            for jh in range(CHUNK // N1):
+                bank = ps1.tile([P, PACK, N1], F32, name="bank")
+                j0 = CHUNK * c + N1 * jh
+                for t in range(PACK):
+                    col4 = 256 * t + P * b
+                    nc.tensor.matmul_mx(
+                        out=bank[:, t, :],
+                        lhsT=w1_codes[b][:, P * t : P * (t + 1)].bitcast(FP8X4),
+                        lhsT_scale=w1_sc[b][:, P * t : P * (t + 1)],
+                        rhs=v0[:, j0 : j0 + N1].bitcast(FP8X4),
+                        rhs_scale=v_sc[PASS0_ROW:, j0 : j0 + N1],
+                        start=True,
+                        stop=False,
+                    )
+                    nc.tensor.matmul_mx(
+                        out=bank[:, t, :],
+                        lhsT=w4_codes[:, 2 * col4 : 2 * (col4 + P)].bitcast(FP4X4),
+                        lhsT_scale=w4_sc[:, col4 : col4 + P],
+                        rhs=v1[c][:, N1 * jh : N1 * (jh + 1)].bitcast(FP8X4),
+                        rhs_scale=v_sc[:, j0 : j0 + N1],
+                        start=False,
+                        stop=True,
+                    )
+                h = bank[:].rearrange("p t n -> p n t")
+                cols = slice(N1 * jh, N1 * (jh + 1))
+                if direct:
+                    nc.scalar.activation(out=act[:, 0, cols, :], in_=h, func=ACT.Relu)
+                    nc.scalar.activation(out=act[:, 1, cols, :], in_=h, func=ACT.Relu, scale=-1.0)
+                else:
+                    nc.scalar.copy(out=hb[:, cols, :], in_=h)
+            if not direct:
+                flat = hb[:].rearrange("p n t -> p (n t)")
+                nc.vector.tensor_scalar(out=act[:, 0].rearrange("p n t -> p (n t)"), in0=flat, scalar1=0.0, scalar2=None, op0=ALU.max)
+                nc.vector.tensor_scalar(out=act[:, 1].rearrange("p n t -> p (n t)"), in0=flat, scalar1=-1.0, scalar2=0.0, op0=ALU.mult, op1=ALU.max)
+            codes = keep.tile([P, 2 * CHUNK], U32, name="act_codes%d_%d" % (c, b), align_bytes=64)
+            sc = keep.tile([P, 2 * CHUNK], U8, name="act_sc%d_%d" % (c, b), align_bytes=64)
+            nc.vector.quantize_mx(out=codes[:].bitcast(FP8X4), scales=sc[:], in_=act[:].rearrange("p s n t -> p (s n t)"))
+            act_codes[c, b] = codes
+            act_sc[c, b] = sc
+
+        def stage2(c):
+            for pair in range(2):
+                banks = [ps2.tile([P, 2, CHUNK], F32, name="e_up"), ps2.tile([P, 2, CHUNK], F32, name="e_down")]
+                for s in range(2):
+                    for i in range(2):
+                        m0 = P * (2 * pair + i)
+                        for b in range(2):
+                            nc.tensor.matmul_mx(
+                                out=banks[s][:, i, :],
+                                lhsT=u[b][:, m0 : m0 + P].bitcast(FP8X4),
+                                lhsT_scale=u_sc[PASS0_ROW * (1 - b) :, m0 : m0 + P],
+                                rhs=act_codes[c, b][:, CHUNK * s : CHUNK * (s + 1)].bitcast(FP8X4),
+                                rhs_scale=act_sc[c, b][:, CHUNK * s : CHUNK * (s + 1)],
+                                start=(b == 0),
+                                stop=(b == 1),
+                            )
+                e_up = ring.tile([P, 2, CHUNK], F32, name="e_up_sb")
+                nc.scalar.copy(out=e_up[:], in_=banks[0][:])
+                best = ring.tile([P, 2, CHUNK], F32, name="best")
+                nc.vector.tensor_tensor(out=best[:], in0=banks[1][:], in1=e_up[:], op=ALU.max)
+                res = ring.tile([P, 2, CHUNK], F32, name="res")
+                for i in range(2):
+                    g = 2 * pair + i
+                    nc.vector.scalar_tensor_tensor(out=res[:, i, :], in0=best[:, i, :], scalar=gains[:, g : g + 1], in1=tri[c][:, g, :], op0=ALU.mult, op1=ALU.add)
+                nc.sync.dma_start(
+                    out=out[2 * P * pair : 2 * P * (pair + 1), CHUNK * c : CHUNK * (c + 1)].rearrange("(g p) j -> p g j", p=P),
+                    in_=res[:],
+                )
+
+        def gather_v1(c):
+            gather(v1[c][:], tab[1][:].bitcast(U32), reeds[:, 16 * c : 16 * (c + 1)])
+
+        nc.vector.tensor_copy(
+            out=w4_codes[:].bitcast(U16).rearrange("p (t m) -> p m t", t=PACK),
+            in_=w4_raw[:].bitcast(U16).rearrange("p (m t) -> p m t", t=PACK),
+        )
+        gather(v0[:], tab[0][:].bitcast(U32), reeds[:])
+        gather(u[0][:], tab[0][:].bitcast(U32), mouths[:])
+        gather(v_sc[:], tab_sc[:], reeds[:])
+        for i in range(4):
+            cast_w1(i)
+        quant_w1(0)
+        gather(u_sc[:], tab_sc[:], mouths[:])
+        quant_w1(1)
+        nc.vector.tensor_copy(
+            out=w4_sc[:].rearrange("p (t m) -> p m t", t=PACK),
+            in_=w4_sc_raw[:].rearrange("p (m t) -> p m t", t=PACK),
+        )
+        gather_v1(0)
+        gather_v1(1)
+        stage1(0, 0)
+        stage1(0, 1)
+        gather(u[1][:], tab[1][:].bitcast(U32), mouths[:])
+        gather_v1(2)
+        gather_v1(3)
+        stage1(1, 0)
+        stage1(1, 1)
+        stage2(0)
+        stage1(2, 0)
+        stage1(2, 1)
+        stage2(1)
+        stage1(3, 0)
+        stage1(3, 1)
+        stage2(2)
+        stage2(3)

@@ -18,15 +18,17 @@ ALU = mybir.AluOpType
 
 P = 128
 PACK = 4
-CHUNK = 256
+CHUNKS = (256, 256, 256, 256)
+GATHER = 256
 N1 = 128
 PASS0_ROW = 4
-DIRECT = ((0, 0), (1, 0), (2, 0), (3, 0))
+DIRECT = ((0, 0), (1, 0), (2, 0), (3, 0), )
 
 
 def tile_list_reed_mouthpiece_fit_kernel(tc, tab_words, tab_scales, offs, offs2, w1, w4_words, w4_scales, gain, trials, out):
     nc = tc.nc
-    n_chunks = S // CHUNK
+    n_chunks = len(CHUNKS)
+    starts = [sum(CHUNKS[:c]) for c in range(n_chunks)]
     with ExitStack() as ctx:
         keep = ctx.enter_context(tc.tile_pool(name="keep", bufs=1))
         ring = ctx.enter_context(tc.tile_pool(name="ring", bufs=4))
@@ -46,12 +48,12 @@ def tile_list_reed_mouthpiece_fit_kernel(tc, tab_words, tab_scales, offs, offs2,
         w1_codes = [keep.tile([P, 512], U32, name="w1_codes%d" % b, align_bytes=64) for b in range(2)]
         w1_sc = [keep.tile([P, 512], U8, name="w1_sc%d" % b, align_bytes=64) for b in range(2)]
         v0 = keep.tile([P, S], U32, name="v0", align_bytes=64)
-        v1 = [keep.tile([P, CHUNK], U32, name="v1_%d" % c, align_bytes=64) for c in range(n_chunks)]
+        v1 = [keep.tile([P, GATHER], U32, name="v1_%d" % c, align_bytes=64) for c in range(S // GATHER)]
         v_sc = keep.tile([P, S], U8, name="v_sc", align_bytes=64)
         u = [keep.tile([P, S2], U32, name="u%d" % a, align_bytes=64) for a in range(2)]
         u_sc = keep.tile([P, S2], U8, name="u_sc", align_bytes=64)
         gains = keep.tile([P, 4], F32, name="gains")
-        tri = [keep.tile([P, 4, CHUNK], F32, name="tri%d" % c) for c in range(n_chunks)]
+        tri = [keep.tile([P, 4, CHUNKS[c]], F32, name="tri%d" % c) for c in range(n_chunks)]
         warm = keep.tile([P, 2], F32, name="warm")
 
         nc.vector.memset(tab_sc[:].bitcast(I32), 0)
@@ -70,24 +72,38 @@ def tile_list_reed_mouthpiece_fit_kernel(tc, tab_words, tab_scales, offs, offs2,
             nc.sync.dma_start(out=w1_raw[i][:], in_=w1[:, 256 * i : 256 * (i + 1)].rearrange("(p j) c -> p j c", j=PACK))
 
         def load_trials(c):
-            nc.sync.dma_start(out=tri[c][:], in_=trials[:, CHUNK * c : CHUNK * (c + 1)].rearrange("(g p) j -> p g j", p=P))
+            nc.sync.dma_start(out=tri[c][:], in_=trials[:, starts[c] : starts[c] + CHUNKS[c]].rearrange("(g p) j -> p g j", p=P))
 
+        def load_scale_row(tile, first_row, rows, r):
+            nc.sync.dma_start(out=tile[first_row + r : P : 32, :].bitcast(I32), in_=rows[r:16:4, :].bitcast(I32))
+
+        load_table(0)
         nc.sync.dma_start(reeds[:], offs)
         nc.sync.dma_start(out=w4_raw[:].bitcast(I32), in_=w4_words[0].bitcast(I32))
-        load_table(0)
-        load_scale_rows(nc.sync, tab_sc, PASS0_ROW, tab_scales[0])
         load_w1(0)
-        nc.sync.dma_start(mouths[:], offs2)
+        load_scale_row(tab_sc, PASS0_ROW, tab_scales[0], 0)
+        load_scale_row(tab_sc, PASS0_ROW, tab_scales[0], 1)
+        load_scale_row(tab_sc, PASS0_ROW, tab_scales[0], 2)
+        load_scale_row(tab_sc, PASS0_ROW, tab_scales[0], 3)
         load_w1(1)
-        load_scale_rows(nc.sync, tab_sc, 0, tab_scales[1])
+        load_scale_row(tab_sc, 0, tab_scales[1], 0)
+        load_scale_row(tab_sc, 0, tab_scales[1], 1)
+        load_scale_row(tab_sc, 0, tab_scales[1], 2)
+        load_scale_row(tab_sc, 0, tab_scales[1], 3)
         load_w1(2)
         load_w1(3)
-        load_scale_rows(nc.sync, w4_sc_raw, 0, w4_scales[0])
+        load_scale_row(w4_sc_raw, 0, w4_scales[0], 0)
+        load_scale_row(w4_sc_raw, 0, w4_scales[0], 1)
+        load_scale_row(w4_sc_raw, 0, w4_scales[0], 2)
+        load_scale_row(w4_sc_raw, 0, w4_scales[0], 3)
         load_table(1)
+        nc.sync.dma_start(mouths[:], offs2)
         with nc.allow_non_contiguous_dma(reason="one gain for each partition"):
             nc.sync.dma_start(out=gains[:], in_=gain.rearrange("(g p) -> p g", p=P))
-        for c in range(n_chunks):
-            load_trials(c)
+        load_trials(0)
+        load_trials(1)
+        load_trials(2)
+        load_trials(3)
 
 
         def cast_w1(i):
@@ -107,13 +123,14 @@ def tile_list_reed_mouthpiece_fit_kernel(tc, tab_words, tab_scales, offs, offs2,
         act_sc = {}
 
         def stage1(c, b):
+            CHUNK = CHUNKS[c]
             act = ring.tile([P, 2, CHUNK, PACK], BF16, name="act", align_bytes=64)
             direct = (c, b) in DIRECT
             if not direct:
                 hb = ring.tile([P, CHUNK, PACK], BF16, name="hb", align_bytes=64)
             for jh in range(CHUNK // N1):
                 bank = ps1.tile([P, PACK, N1], F32, name="bank")
-                j0 = CHUNK * c + N1 * jh
+                j0 = starts[c] + N1 * jh
                 for t in range(PACK):
                     col4 = 256 * t + P * b
                     nc.tensor.matmul_mx(
@@ -129,7 +146,7 @@ def tile_list_reed_mouthpiece_fit_kernel(tc, tab_words, tab_scales, offs, offs2,
                         out=bank[:, t, :],
                         lhsT=w4_codes[:, 2 * col4 : 2 * (col4 + P)].bitcast(FP4X4),
                         lhsT_scale=w4_sc[:, col4 : col4 + P],
-                        rhs=v1[c][:, N1 * jh : N1 * (jh + 1)].bitcast(FP8X4),
+                        rhs=v1[j0 // GATHER][:, j0 % GATHER : j0 % GATHER + N1].bitcast(FP8X4),
                         rhs_scale=v_sc[:, j0 : j0 + N1],
                         start=False,
                         stop=True,
@@ -152,11 +169,13 @@ def tile_list_reed_mouthpiece_fit_kernel(tc, tab_words, tab_scales, offs, offs2,
             act_sc[c, b] = sc
 
         def stage2(c):
-            for pair in range(2):
-                banks = [ps2.tile([P, 2, CHUNK], F32, name="e_up"), ps2.tile([P, 2, CHUNK], F32, name="e_down")]
+            CHUNK = CHUNKS[c]
+            per_bank = 512 // CHUNK
+            for g0 in range(0, 4, per_bank):
+                banks = [ps2.tile([P, per_bank, CHUNK], F32, name="e_up"), ps2.tile([P, per_bank, CHUNK], F32, name="e_down")]
                 for s in range(2):
-                    for i in range(2):
-                        m0 = P * (2 * pair + i)
+                    for i in range(per_bank):
+                        m0 = P * (g0 + i)
                         for b in range(2):
                             nc.tensor.matmul_mx(
                                 out=banks[s][:, i, :],
@@ -167,45 +186,47 @@ def tile_list_reed_mouthpiece_fit_kernel(tc, tab_words, tab_scales, offs, offs2,
                                 start=(b == 0),
                                 stop=(b == 1),
                             )
-                e_up = ring.tile([P, 2, CHUNK], F32, name="e_up_sb")
+                e_up = ring.tile([P, per_bank, CHUNK], F32, name="e_up_sb")
                 nc.scalar.copy(out=e_up[:], in_=banks[0][:])
-                best = ring.tile([P, 2, CHUNK], F32, name="best")
+                best = ring.tile([P, per_bank, CHUNK], F32, name="best")
                 nc.vector.tensor_tensor(out=best[:], in0=banks[1][:], in1=e_up[:], op=ALU.max)
-                res = ring.tile([P, 2, CHUNK], F32, name="res")
-                for i in range(2):
-                    g = 2 * pair + i
+                res = ring.tile([P, per_bank, CHUNK], F32, name="res")
+                for i in range(per_bank):
+                    g = g0 + i
                     nc.vector.scalar_tensor_tensor(out=res[:, i, :], in0=best[:, i, :], scalar=gains[:, g : g + 1], in1=tri[c][:, g, :], op0=ALU.mult, op1=ALU.add)
                 nc.sync.dma_start(
-                    out=out[2 * P * pair : 2 * P * (pair + 1), CHUNK * c : CHUNK * (c + 1)].rearrange("(g p) j -> p g j", p=P),
+                    out=out[P * g0 : P * (g0 + per_bank), starts[c] : starts[c] + CHUNK].rearrange("(g p) j -> p g j", p=P),
                     in_=res[:],
                 )
 
         def gather_v1(c):
             gather(v1[c][:], tab[1][:].bitcast(U32), reeds[:, 16 * c : 16 * (c + 1)])
 
-        nc.vector.tensor_copy(
-            out=w4_codes[:].bitcast(U16).rearrange("p (t m) -> p m t", t=PACK),
-            in_=w4_raw[:].bitcast(U16).rearrange("p (m t) -> p m t", t=PACK),
-        )
         gather(v0[:], tab[0][:].bitcast(U32), reeds[:])
-        gather(u[0][:], tab[0][:].bitcast(U32), mouths[:])
-        gather(v_sc[:], tab_sc[:], reeds[:])
-        for i in range(4):
-            cast_w1(i)
-        quant_w1(0)
-        gather(u_sc[:], tab_sc[:], mouths[:])
-        quant_w1(1)
         nc.vector.tensor_copy(
-            out=w4_sc[:].rearrange("p (t m) -> p m t", t=PACK),
-            in_=w4_sc_raw[:].rearrange("p (m t) -> p m t", t=PACK),
+            out=w4_codes[:].bitcast(U16).rearrange("p (t m) -> p t m", t=PACK),
+            in_=w4_raw[:].bitcast(U16).rearrange("p (m t) -> p t m", t=PACK),
         )
+        gather(v_sc[:], tab_sc[:], reeds[:])
+        cast_w1(0)
+        cast_w1(1)
+        cast_w1(2)
+        cast_w1(3)
+        quant_w1(0)
+        nc.vector.tensor_copy(
+            out=w4_sc[:].rearrange("p (t m) -> p t m", t=PACK),
+            in_=w4_sc_raw[:].rearrange("p (m t) -> p t m", t=PACK),
+        )
+        quant_w1(1)
         gather_v1(0)
         gather_v1(1)
         stage1(0, 0)
         stage1(0, 1)
-        gather(u[1][:], tab[1][:].bitcast(U32), mouths[:])
         gather_v1(2)
         gather_v1(3)
+        gather(u[0][:], tab[0][:].bitcast(U32), mouths[:])
+        gather(u_sc[:], tab_sc[:], mouths[:])
+        gather(u[1][:], tab[1][:].bitcast(U32), mouths[:])
         stage1(1, 0)
         stage1(1, 1)
         stage2(0)

@@ -22,7 +22,7 @@ CHUNKS = (256, 256, 256, 256)
 GATHER = 256
 N1 = 128
 PASS0_ROW = 4
-DIRECT = ((0, 0), (1, 0), (2, 0), (3, 0), )
+DIRECT = ((1, 1), (2, 1), (3, 1), )
 
 
 def tile_list_reed_mouthpiece_fit_kernel(tc, tab_words, tab_scales, offs, offs2, w1, w4_words, w4_scales, gain, trials, out):
@@ -43,7 +43,7 @@ def tile_list_reed_mouthpiece_fit_kernel(tc, tab_words, tab_scales, offs, offs2,
         w4_sc_raw = keep.tile([P, K], U8, name="w4_sc_raw", align_bytes=64)
         w4_codes = keep.tile([P, 2 * K], U8, name="w4_codes", align_bytes=64)
         w4_sc = keep.tile([P, K], U8, name="w4_sc", align_bytes=64)
-        w1_raw = [keep.tile([P, PACK, 256], F32, name="w1_raw%d" % i) for i in range(4)]
+        w1_raw = [keep.tile([P, PACK, 512], F32, name="w1_raw%d" % i) for i in range(2)]
         w1_bf = [keep.tile([P, PACK, P, PACK], BF16, name="w1_bf%d" % b, align_bytes=64) for b in range(2)]
         w1_codes = [keep.tile([P, 512], U32, name="w1_codes%d" % b, align_bytes=64) for b in range(2)]
         w1_sc = [keep.tile([P, 512], U8, name="w1_sc%d" % b, align_bytes=64) for b in range(2)]
@@ -69,7 +69,7 @@ def tile_list_reed_mouthpiece_fit_kernel(tc, tab_words, tab_scales, offs, offs2,
                 queue.dma_start(out=tile[first_row + r : P : 32, :].bitcast(I32), in_=rows[r:16:4, :].bitcast(I32))
 
         def load_w1(i):
-            nc.sync.dma_start(out=w1_raw[i][:], in_=w1[:, 256 * i : 256 * (i + 1)].rearrange("(p j) c -> p j c", j=PACK))
+            nc.sync.dma_start(out=w1_raw[i][:], in_=w1[:, 512 * i : 512 * (i + 1)].rearrange("(p j) c -> p j c", j=PACK))
 
         def load_trials(c):
             nc.sync.dma_start(out=tri[c][:], in_=trials[:, starts[c] : starts[c] + CHUNKS[c]].rearrange("(g p) j -> p g j", p=P))
@@ -79,25 +79,23 @@ def tile_list_reed_mouthpiece_fit_kernel(tc, tab_words, tab_scales, offs, offs2,
 
         load_table(0)
         nc.sync.dma_start(reeds[:], offs)
+        nc.sync.dma_start(mouths[:], offs2)
         nc.sync.dma_start(out=w4_raw[:].bitcast(I32), in_=w4_words[0].bitcast(I32))
-        load_w1(0)
         load_scale_row(tab_sc, PASS0_ROW, tab_scales[0], 0)
         load_scale_row(tab_sc, PASS0_ROW, tab_scales[0], 1)
         load_scale_row(tab_sc, PASS0_ROW, tab_scales[0], 2)
+        load_w1(0)
         load_scale_row(tab_sc, PASS0_ROW, tab_scales[0], 3)
-        load_w1(1)
         load_scale_row(tab_sc, 0, tab_scales[1], 0)
         load_scale_row(tab_sc, 0, tab_scales[1], 1)
         load_scale_row(tab_sc, 0, tab_scales[1], 2)
         load_scale_row(tab_sc, 0, tab_scales[1], 3)
-        load_w1(2)
-        load_w1(3)
         load_scale_row(w4_sc_raw, 0, w4_scales[0], 0)
+        load_w1(1)
         load_scale_row(w4_sc_raw, 0, w4_scales[0], 1)
         load_scale_row(w4_sc_raw, 0, w4_scales[0], 2)
         load_scale_row(w4_sc_raw, 0, w4_scales[0], 3)
         load_table(1)
-        nc.sync.dma_start(mouths[:], offs2)
         with nc.allow_non_contiguous_dma(reason="one gain for each partition"):
             nc.sync.dma_start(out=gains[:], in_=gain.rearrange("(g p) -> p g", p=P))
         load_trials(0)
@@ -106,12 +104,8 @@ def tile_list_reed_mouthpiece_fit_kernel(tc, tab_words, tab_scales, offs, offs2,
         load_trials(3)
 
 
-        def cast_w1(i):
-            b, half = divmod(i, 2)
-            nc.scalar.copy(
-                out=w1_bf[b][:, :, 64 * half : 64 * (half + 1), :].rearrange("p t m j -> p m j t"),
-                in_=w1_raw[i][:].rearrange("p j (m t) -> p m j t", t=PACK),
-            )
+        def cast_w1(b):
+            nc.scalar.copy(out=w1_bf[b][:].rearrange("p t m j -> p m j t"), in_=w1_raw[b][:].rearrange("p j (m t) -> p m j t", t=PACK))
 
         def quant_w1(b):
             nc.vector.quantize_mx(out=w1_codes[b][:].bitcast(FP8X4), scales=w1_sc[b][:], in_=w1_bf[b][:].rearrange("p t m j -> p (t m j)"))
@@ -132,16 +126,17 @@ def tile_list_reed_mouthpiece_fit_kernel(tc, tab_words, tab_scales, offs, offs2,
                 bank = ps1.tile([P, PACK, N1], F32, name="bank")
                 j0 = starts[c] + N1 * jh
                 for t in range(PACK):
-                    col4 = 256 * t + P * b
                     nc.tensor.matmul_mx(
                         out=bank[:, t, :],
                         lhsT=w1_codes[b][:, P * t : P * (t + 1)].bitcast(FP8X4),
                         lhsT_scale=w1_sc[b][:, P * t : P * (t + 1)],
                         rhs=v0[:, j0 : j0 + N1].bitcast(FP8X4),
                         rhs_scale=v_sc[PASS0_ROW:, j0 : j0 + N1],
-                        start=True,
+                        start=(t == 0),
                         stop=False,
                     )
+                for t in range(PACK):
+                    col4 = 256 * t + P * b
                     nc.tensor.matmul_mx(
                         out=bank[:, t, :],
                         lhsT=w4_codes[:, 2 * col4 : 2 * (col4 + P)].bitcast(FP4X4),
@@ -149,7 +144,7 @@ def tile_list_reed_mouthpiece_fit_kernel(tc, tab_words, tab_scales, offs, offs2,
                         rhs=v1[j0 // GATHER][:, j0 % GATHER : j0 % GATHER + N1].bitcast(FP8X4),
                         rhs_scale=v_sc[:, j0 : j0 + N1],
                         start=False,
-                        stop=True,
+                        stop=(t == PACK - 1),
                     )
                 h = bank[:].rearrange("p t n -> p n t")
                 cols = slice(N1 * jh, N1 * (jh + 1))
@@ -191,18 +186,23 @@ def tile_list_reed_mouthpiece_fit_kernel(tc, tab_words, tab_scales, offs, offs2,
                 best = ring.tile([P, per_bank, CHUNK], F32, name="best")
                 nc.vector.tensor_tensor(out=best[:], in0=banks[1][:], in1=e_up[:], op=ALU.max)
                 res = ring.tile([P, per_bank, CHUNK], F32, name="res")
+                last = c == n_chunks - 1
                 for i in range(per_bank):
                     g = g0 + i
                     nc.vector.scalar_tensor_tensor(out=res[:, i, :], in0=best[:, i, :], scalar=gains[:, g : g + 1], in1=tri[c][:, g, :], op0=ALU.mult, op1=ALU.add)
-                nc.sync.dma_start(
-                    out=out[P * g0 : P * (g0 + per_bank), starts[c] : starts[c] + CHUNK].rearrange("(g p) j -> p g j", p=P),
-                    in_=res[:],
-                )
+                    if last:
+                        nc.sync.dma_start(out=out[P * g : P * (g + 1), starts[c] : starts[c] + CHUNK], in_=res[:, i, :])
+                if not last:
+                    nc.sync.dma_start(
+                        out=out[P * g0 : P * (g0 + per_bank), starts[c] : starts[c] + CHUNK].rearrange("(g p) j -> p g j", p=P),
+                        in_=res[:],
+                    )
 
         def gather_v1(c):
             gather(v1[c][:], tab[1][:].bitcast(U32), reeds[:, 16 * c : 16 * (c + 1)])
 
         gather(v0[:], tab[0][:].bitcast(U32), reeds[:])
+        gather(u[0][:], tab[0][:].bitcast(U32), mouths[:])
         nc.vector.tensor_copy(
             out=w4_codes[:].bitcast(U16).rearrange("p (t m) -> p t m", t=PACK),
             in_=w4_raw[:].bitcast(U16).rearrange("p (m t) -> p t m", t=PACK),
@@ -210,30 +210,27 @@ def tile_list_reed_mouthpiece_fit_kernel(tc, tab_words, tab_scales, offs, offs2,
         gather(v_sc[:], tab_sc[:], reeds[:])
         cast_w1(0)
         cast_w1(1)
-        cast_w1(2)
-        cast_w1(3)
         quant_w1(0)
+        gather(u_sc[:], tab_sc[:], mouths[:])
         nc.vector.tensor_copy(
             out=w4_sc[:].rearrange("p (t m) -> p t m", t=PACK),
             in_=w4_sc_raw[:].rearrange("p (m t) -> p t m", t=PACK),
         )
-        quant_w1(1)
         gather_v1(0)
+        quant_w1(1)
         gather_v1(1)
         stage1(0, 0)
         stage1(0, 1)
+        gather(u[1][:], tab[1][:].bitcast(U32), mouths[:])
         gather_v1(2)
         gather_v1(3)
-        gather(u[0][:], tab[0][:].bitcast(U32), mouths[:])
-        gather(u_sc[:], tab_sc[:], mouths[:])
-        gather(u[1][:], tab[1][:].bitcast(U32), mouths[:])
         stage1(1, 0)
         stage1(1, 1)
-        stage2(0)
         stage1(2, 0)
+        stage2(0)
         stage1(2, 1)
-        stage2(1)
         stage1(3, 0)
+        stage2(1)
         stage1(3, 1)
         stage2(2)
         stage2(3)

@@ -22,7 +22,7 @@ CHUNKS = (256, 256, 256, 256)
 GATHER = 256
 N1 = 128
 PASS0_ROW = 4
-DIRECT = ((1, 1), (2, 1), (3, 1), )
+DIRECT = ((2, 1), (3, 1), )
 
 
 def tile_list_reed_mouthpiece_fit_kernel(tc, tab_words, tab_scales, offs, offs2, w1, w4_words, w4_scales, gain, trials, out):
@@ -159,7 +159,12 @@ def tile_list_reed_mouthpiece_fit_kernel(tc, tab_words, tab_scales, offs, offs2,
                 nc.vector.tensor_scalar(out=act[:, 1].rearrange("p n t -> p (n t)"), in0=flat, scalar1=-1.0, scalar2=0.0, op0=ALU.mult, op1=ALU.max)
             codes = keep.tile([P, 2 * CHUNK], U32, name="act_codes%d_%d" % (c, b), align_bytes=64)
             sc = keep.tile([P, 2 * CHUNK], U8, name="act_sc%d_%d" % (c, b), align_bytes=64)
-            nc.vector.quantize_mx(out=codes[:].bitcast(FP8X4), scales=sc[:], in_=act[:].rearrange("p s n t -> p (s n t)"))
+            if direct:
+                nc.vector.quantize_mx(out=codes[:].bitcast(FP8X4), scales=sc[:], in_=act[:].rearrange("p s n t -> p (s n t)"))
+            else:
+                for s in range(2):
+                    half = slice(CHUNK * s, CHUNK * (s + 1))
+                    nc.vector.quantize_mx(out=codes[:, half].bitcast(FP8X4), scales=sc[:, half], in_=act[:, s].rearrange("p n t -> p (n t)"))
             act_codes[c, b] = codes
             act_sc[c, b] = sc
 

from contextlib import ExitStack

import concourse.mybir as mybir

K, KC, T, S, S2 = 1024, 512, 2048, 1024, 512
FLOPS = 2 * K * K * S + 2 * 2 * K * S2 * S

F32 = mybir.dt.float32
BF16 = mybir.dt.bfloat16
I32 = mybir.dt.int32
U32 = mybir.dt.uint32
U16 = mybir.dt.uint16
U8 = mybir.dt.uint8
FP8X4 = mybir.dt.float8_e4m3fn_x4
FP4X4 = mybir.dt.float4_e2m1fn_x4
ACT = mybir.ActivationFunctionType
ALU = mybir.AluOpType

P = 128
PACK = 4
CHUNKS = (256, 256, 256, 256)
GATHER = 256
N1 = 128
PASS0_ROW = 4
DIRECT = ((2, 1), (3, 1), )


def tile_list_reed_mouthpiece_fit_kernel(tc, tab_words, tab_scales, offs, offs2, w1, w4_words, w4_scales, gain, trials, out):
    nc = tc.nc
    n_chunks = len(CHUNKS)
    starts = [sum(CHUNKS[:c]) for c in range(n_chunks)]
    with ExitStack() as ctx:
        keep = ctx.enter_context(tc.tile_pool(name="keep", bufs=1))
        ring = ctx.enter_context(tc.tile_pool(name="ring", bufs=4))
        ps1 = ctx.enter_context(tc.psum_pool(name="ps1", bufs=4))
        ps2 = ctx.enter_context(tc.psum_pool(name="ps2", bufs=2))

        reeds = keep.tile([P, S // 16], U16, name="reeds")
        mouths = keep.tile([P, S2 // 16], U16, name="mouths")
        tab = [keep.tile([P, T], I32, name="tab%d" % a, align_bytes=64) for a in range(2)]
        tab_sc = keep.tile([P, T], U8, name="tab_sc", align_bytes=64)
        w4_raw = keep.tile([P, 2 * K], U8, name="w4_raw", align_bytes=64)
        w4_sc_raw = keep.tile([P, K], U8, name="w4_sc_raw", align_bytes=64)
        w4_codes = keep.tile([P, 2 * K], U8, name="w4_codes", align_bytes=64)
        w4_sc = keep.tile([P, K], U8, name="w4_sc", align_bytes=64)
        w1_raw = [keep.tile([P, PACK, 512], F32, name="w1_raw%d" % i) for i in range(2)]
        w1_bf = [keep.tile([P, PACK, P, PACK], BF16, name="w1_bf%d" % b, align_bytes=64) for b in range(2)]
        w1_codes = [keep.tile([P, 512], U32, name="w1_codes%d" % b, align_bytes=64) for b in range(2)]
        w1_sc = [keep.tile([P, 512], U8, name="w1_sc%d" % b, align_bytes=64) for b in range(2)]
        v0 = keep.tile([P, S], U32, name="v0", align_bytes=64)
        v1 = [keep.tile([P, GATHER], U32, name="v1_%d" % c, align_bytes=64) for c in range(S // GATHER)]
        v_sc = keep.tile([P, S], U8, name="v_sc", align_bytes=64)
        u = [keep.tile([P, S2], U32, name="u%d" % a, align_bytes=64) for a in range(2)]
        u_sc = keep.tile([P, S2], U8, name="u_sc", align_bytes=64)
        gains = keep.tile([P, 4], F32, name="gains")
        tri = [keep.tile([P, 4, CHUNKS[c]], F32, name="tri%d" % c) for c in range(n_chunks)]
        warm = keep.tile([P, 2], F32, name="warm")

        nc.vector.memset(tab_sc[:].bitcast(I32), 0)
        nc.vector.memset(w4_sc_raw[:].bitcast(I32), 0)
        nc.vector.memset(warm[:, 0:1], 0.0)
        nc.scalar.activation(out=warm[:, 1:2], in_=warm[:, 0:1], func=ACT.Relu)

        def load_table(a):
            nc.sync.dma_start(out=tab[a][:], in_=tab_words[a].rearrange("p n t -> p (n t)").bitcast(I32))

        def load_scale_rows(queue, tile, first_row, rows):
            for r in range(4):
                queue.dma_start(out=tile[first_row + r : P : 32, :].bitcast(I32), in_=rows[r:16:4, :].bitcast(I32))

        def load_w1(i):
            nc.sync.dma_start(out=w1_raw[i][:], in_=w1[:, 512 * i : 512 * (i + 1)].rearrange("(p j) c -> p j c", j=PACK))

        def load_trials(c):
            nc.sync.dma_start(out=tri[c][:], in_=trials[:, starts[c] : starts[c] + CHUNKS[c]].rearrange("(g p) j -> p g j", p=P))

        def load_scale_row(tile, first_row, rows, r):
            nc.sync.dma_start(out=tile[first_row + r : P : 32, :].bitcast(I32), in_=rows[r:16:4, :].bitcast(I32))

        load_table(0)
        nc.sync.dma_start(reeds[:], offs)
        nc.sync.dma_start(mouths[:], offs2)
        nc.sync.dma_start(out=w4_raw[:].bitcast(I32), in_=w4_words[0].bitcast(I32))
        load_scale_row(tab_sc, PASS0_ROW, tab_scales[0], 0)
        load_scale_row(tab_sc, PASS0_ROW, tab_scales[0], 1)
        load_scale_row(tab_sc, PASS0_ROW, tab_scales[0], 2)
        load_w1(0)
        load_scale_row(tab_sc, PASS0_ROW, tab_scales[0], 3)
        load_scale_row(tab_sc, 0, tab_scales[1], 0)
        load_scale_row(tab_sc, 0, tab_scales[1], 1)
        load_scale_row(tab_sc, 0, tab_scales[1], 2)
        load_scale_row(tab_sc, 0, tab_scales[1], 3)
        load_scale_row(w4_sc_raw, 0, w4_scales[0], 0)
        load_w1(1)
        load_scale_row(w4_sc_raw, 0, w4_scales[0], 1)
        load_scale_row(w4_sc_raw, 0, w4_scales[0], 2)
        load_scale_row(w4_sc_raw, 0, w4_scales[0], 3)
        load_table(1)
        with nc.allow_non_contiguous_dma(reason="one gain for each partition"):
            nc.sync.dma_start(out=gains[:], in_=gain.rearrange("(g p) -> p g", p=P))
        load_trials(0)
        load_trials(1)
        load_trials(2)
        load_trials(3)


        def cast_w1(b):
            nc.scalar.copy(out=w1_bf[b][:].rearrange("p t m j -> p m j t"), in_=w1_raw[b][:].rearrange("p j (m t) -> p m j t", t=PACK))

        def quant_w1(b):
            nc.vector.quantize_mx(out=w1_codes[b][:].bitcast(FP8X4), scales=w1_sc[b][:], in_=w1_bf[b][:].rearrange("p t m j -> p (t m j)"))

        def gather(dst, window, offsets):
            nc.vector.tensor_copy(out=dst, in_=window.indirect(offsets))

        act_codes = {}
        act_sc = {}

        def stage1(c, b):
            CHUNK = CHUNKS[c]
            act = ring.tile([P, 2, CHUNK, PACK], BF16, name="act", align_bytes=64)
            direct = (c, b) in DIRECT
            if not direct:
                hb = ring.tile([P, CHUNK, PACK], BF16, name="hb", align_bytes=64)
            for jh in range(CHUNK // N1):
                bank = ps1.tile([P, PACK, N1], F32, name="bank")
                j0 = starts[c] + N1 * jh
                for t in range(PACK):
                    nc.tensor.matmul_mx(
                        out=bank[:, t, :],
                        lhsT=w1_codes[b][:, P * t : P * (t + 1)].bitcast(FP8X4),
                        lhsT_scale=w1_sc[b][:, P * t : P * (t + 1)],
                        rhs=v0[:, j0 : j0 + N1].bitcast(FP8X4),
                        rhs_scale=v_sc[PASS0_ROW:, j0 : j0 + N1],
                        start=(t == 0),
                        stop=False,
                    )
                for t in range(PACK):
                    col4 = 256 * t + P * b
                    nc.tensor.matmul_mx(
                        out=bank[:, t, :],
                        lhsT=w4_codes[:, 2 * col4 : 2 * (col4 + P)].bitcast(FP4X4),
                        lhsT_scale=w4_sc[:, col4 : col4 + P],
                        rhs=v1[j0 // GATHER][:, j0 % GATHER : j0 % GATHER + N1].bitcast(FP8X4),
                        rhs_scale=v_sc[:, j0 : j0 + N1],
                        start=False,
                        stop=(t == PACK - 1),
                    )
                h = bank[:].rearrange("p t n -> p n t")
                cols = slice(N1 * jh, N1 * (jh + 1))
                if direct:
                    nc.scalar.activation(out=act[:, 0, cols, :], in_=h, func=ACT.Relu)
                    nc.scalar.activation(out=act[:, 1, cols, :], in_=h, func=ACT.Relu, scale=-1.0)
                else:
                    nc.scalar.copy(out=hb[:, cols, :], in_=h)
            if not direct:
                flat = hb[:].rearrange("p n t -> p (n t)")
                nc.vector.tensor_scalar(out=act[:, 0].rearrange("p n t -> p (n t)"), in0=flat, scalar1=0.0, scalar2=None, op0=ALU.max)
                nc.vector.tensor_scalar(out=act[:, 1].rearrange("p n t -> p (n t)"), in0=flat, scalar1=-1.0, scalar2=0.0, op0=ALU.mult, op1=ALU.max)
            codes = keep.tile([P, 2 * CHUNK], U32, name="act_codes%d_%d" % (c, b), align_bytes=64)
            sc = keep.tile([P, 2 * CHUNK], U8, name="act_sc%d_%d" % (c, b), align_bytes=64)
            if direct:
                nc.vector.quantize_mx(out=codes[:].bitcast(FP8X4), scales=sc[:], in_=act[:].rearrange("p s n t -> p (s n t)"))
            else:
                for s in range(2):
                    half = slice(CHUNK * s, CHUNK * (s + 1))
                    nc.vector.quantize_mx(out=codes[:, half].bitcast(FP8X4), scales=sc[:, half], in_=act[:, s].rearrange("p n t -> p (n t)"))
            act_codes[c, b] = codes
            act_sc[c, b] = sc

        def stage2(c):
            CHUNK = CHUNKS[c]
            per_bank = 512 // CHUNK
            for g0 in range(0, 4, per_bank):
                banks = [ps2.tile([P, per_bank, CHUNK], F32, name="e_up"), ps2.tile([P, per_bank, CHUNK], F32, name="e_down")]
                for s in range(2):
                    for i in range(per_bank):
                        m0 = P * (g0 + i)
                        for b in range(2):
                            nc.tensor.matmul_mx(
                                out=banks[s][:, i, :],
                                lhsT=u[b][:, m0 : m0 + P].bitcast(FP8X4),
                                lhsT_scale=u_sc[PASS0_ROW * (1 - b) :, m0 : m0 + P],
                                rhs=act_codes[c, b][:, CHUNK * s : CHUNK * (s + 1)].bitcast(FP8X4),
                                rhs_scale=act_sc[c, b][:, CHUNK * s : CHUNK * (s + 1)],
                                start=(b == 0),
                                stop=(b == 1),
                            )
                e_up = ring.tile([P, per_bank, CHUNK], F32, name="e_up_sb")
                nc.scalar.copy(out=e_up[:], in_=banks[0][:])
                best = ring.tile([P, per_bank, CHUNK], F32, name="best")
                nc.vector.tensor_tensor(out=best[:], in0=banks[1][:], in1=e_up[:], op=ALU.max)
                res = ring.tile([P, per_bank, CHUNK], F32, name="res")
                last = c == n_chunks - 1
                for i in range(per_bank):
                    g = g0 + i
                    nc.vector.scalar_tensor_tensor(out=res[:, i, :], in0=best[:, i, :], scalar=gains[:, g : g + 1], in1=tri[c][:, g, :], op0=ALU.mult, op1=ALU.add)
                    if last:
                        nc.sync.dma_start(out=out[P * g : P * (g + 1), starts[c] : starts[c] + CHUNK], in_=res[:, i, :])
                if not last:
                    nc.sync.dma_start(
                        out=out[P * g0 : P * (g0 + per_bank), starts[c] : starts[c] + CHUNK].rearrange("(g p) j -> p g j", p=P),
                        in_=res[:],
                    )

        def gather_v1(c):
            gather(v1[c][:], tab[1][:].bitcast(U32), reeds[:, 16 * c : 16 * (c + 1)])

        gather(v0[:], tab[0][:].bitcast(U32), reeds[:])
        gather(u[0][:], tab[0][:].bitcast(U32), mouths[:])
        nc.vector.tensor_copy(
            out=w4_codes[:].bitcast(U16).rearrange("p (t m) -> p t m", t=PACK),
            in_=w4_raw[:].bitcast(U16).rearrange("p (m t) -> p t m", t=PACK),
        )
        gather(v_sc[:], tab_sc[:], reeds[:])
        cast_w1(0)
        cast_w1(1)
        quant_w1(0)
        gather(u_sc[:], tab_sc[:], mouths[:])
        nc.vector.tensor_copy(
            out=w4_sc[:].rearrange("p (t m) -> p t m", t=PACK),
            in_=w4_sc_raw[:].rearrange("p (m t) -> p t m", t=PACK),
        )
        gather_v1(0)
        quant_w1(1)
        gather_v1(1)
        stage1(0, 0)
        stage1(0, 1)
        gather(u[1][:], tab[1][:].bitcast(U32), mouths[:])
        gather_v1(2)
        gather_v1(3)
        stage1(1, 0)
        stage1(1, 1)
        stage1(2, 0)
        stage2(0)
        stage1(2, 1)
        stage1(3, 0)
        stage2(1)
        stage1(3, 1)
        stage2(2)
        stage2(3)
